import numpy as np
import ml_dtypes


def mxq(x, axis, fmt="e4m3"):
    dtype, down = {"e4m3": (ml_dtypes.float8_e4m3fn, 7), "e5m2": (ml_dtypes.float8_e5m2, 14)}[fmt]
    v = np.moveaxis(np.asarray(x, np.float32).astype(ml_dtypes.bfloat16).astype(np.float64), axis, -1)
    blocks = v.reshape(v.shape[:-1] + (-1, 32))
    amax = np.abs(blocks).max(-1, keepdims=True)
    byte = np.maximum(np.where(amax > 0, np.frexp(amax)[1] - 1 + 127, 0) - down, 1)
    scale = np.exp2(byte - 127.0)
    codes = (blocks / scale).astype(np.float32).astype(dtype).astype(np.float64)
    return np.moveaxis((codes * scale).reshape(v.shape), -1, axis)


WIDE = False


def mx_kscale(k):
    if not WIDE:
        return np.ones(k)
    levels = np.array([10, -10, 5, -5, 0])
    if k % 512:
        return np.exp2(np.random.permutation(np.resize(levels, k // 32))).repeat(32)
    a = np.empty((k // 512, 16))
    for p in range(k // 512):
        a[p, :8] = np.random.permutation(np.resize(levels, 8))
        for g in range(8):
            far = levels[np.abs(levels - a[p, g]) >= 10]
            a[p, g + 8] = far[np.random.randint(len(far))]
    return np.exp2(a.ravel()).repeat(32)


BF16 = ml_dtypes.bfloat16


def bf(x):
    return np.asarray(x, np.float32).astype(BF16)


def f64(x):
    return np.asarray(x).astype(np.float64)


N, DA1, DV1, DT1, H, O = 128, 16, 16, 16, 2048, 2048
DA, DV, DT = DA1 - 1, DV1 - 1, DT1 - 1
Z = DA1 * DV1 * DT1


def prepend_one(x):
    return np.concatenate([np.ones((x.shape[0], 1)), x], axis=-1)


def draw0():
    s, u = mx_kscale(Z), mx_kscale(H)
    return {"a": bf(np.random.standard_normal((N, DA))),
            "v": bf(np.random.standard_normal((N, DV))),
            "t": bf(np.random.standard_normal((N, DT))),
            "gz": bf((1.0 + 0.1 * np.random.standard_normal(Z)) * s),
            "w1": bf(np.random.standard_normal((Z, H)) / np.sqrt(Z) / s[:, None]),
            "gh": bf(np.random.standard_normal(H) * u),
            "w2": bf(1.4 * np.random.standard_normal((H, O)) / np.sqrt(H) / u[:, None])}


def core(a, v, t, gz, w1, gh, w2):
    a1 = prepend_one(f64(a))
    v1 = prepend_one(f64(v))
    t1 = prepend_one(f64(t))
    z4 = a1[:, :, None, None] * v1[:, None, :, None] * t1[:, None, None, :]
    z = z4.reshape(a.shape[0], w1.shape[0])
    zg = z * f64(gz)[None, :]
    p = mxq(zg, 1, "e4m3") @ mxq(f64(w1), 0, "e4m3")
    h = np.maximum(p, 0.0) * f64(gh)[None, :]
    return mxq(h, 1, "e4m3") @ mxq(f64(w2), 0, "e4m3")


def e4m3fn_bytes(y):
    return np.clip(np.asarray(y, np.float64), -448.0, 448.0).astype(np.float32).astype(ml_dtypes.float8_e4m3fn).view(np.uint8)


def e4m3fn_values(b):
    return np.asarray(b, np.uint8).view(ml_dtypes.float8_e4m3fn).astype(np.float64)


def setup_inputs():
    d = draw0()
    x0 = np.asarray(d['w1']).astype(np.float64)
    s = (np.max(np.abs(x0), axis=(1,), keepdims=True) / 448.0).astype(np.float32)
    out = {}
    for k, v in d.items():
        if k == 'w1':
            out['w1_bytes'] = e4m3fn_bytes(x0 / s.astype(np.float64))
            out['w1_scale'] = s
        else:
            out[k] = v
    return out


def reference(a, v, t, gz, w1_bytes, w1_scale, gh, w2):
    return core(a, v, t, gz, e4m3fn_values(w1_bytes) * w1_scale.astype(np.float64), gh, w2)

@@ -1,0 +1,290 @@
+from contextlib import ExitStack
+
+import concourse.mybir as mybir
+from concourse.masks import make_identity
+
+F32 = mybir.dt.float32
+BF16 = mybir.dt.bfloat16
+U32 = mybir.dt.uint32
+U8 = mybir.dt.uint8
+FP8 = mybir.dt.float8_e4m3fn
+FP8X4 = mybir.dt.float8_e4m3fn_x4
+ALU = mybir.AluOpType
+ACT = mybir.ActivationFunctionType
+
+P = 128
+T = 4
+TOK = 128
+Z = 4096
+H = 2048
+O = 2048
+G1 = Z // 512
+G2 = H // 512
+HALF = 1024
+Q = 512
+FLOPS = 2 * TOK * Z * H + 2 * TOK * H * O
+
+V_COLS = 256
+
+
+def tile_tensorfusionouterproducthead_w_kernel(tc, a, v, t, gz, w1_bytes, w1_scale, gh, w2, out):
+    nc = tc.nc
+    with ExitStack() as ctx:
+        keep = ctx.enter_context(tc.tile_pool(name="keep", bufs=1))
+        bytes_pool = ctx.enter_context(tc.tile_pool(name="bytes_pool", bufs=6))
+        wide_pool = ctx.enter_context(tc.tile_pool(name="wide_pool", bufs=3))
+        grp_pool = ctx.enter_context(tc.tile_pool(name="grp_pool", bufs=3))
+        code_pool = ctx.enter_context(tc.tile_pool(name="code_pool", bufs=3))
+        raw_pool = ctx.enter_context(tc.tile_pool(name="raw_pool", bufs=6))
+        psum = ctx.enter_context(tc.psum_pool(name="psum", bufs=1))
+        ctx.enter_context(tc.manual_schedule())
+
+        w1_view = w1_bytes.rearrange("(g p t) n -> g p t n", p=P, t=T)
+        w2_view = w2.rearrange("(g p t) n -> g p t n", p=P, t=T)
+        scale_view = w1_scale.rearrange("(g p t) o -> p g (t o)", p=P, t=T)
+
+        w1s = keep.tile([P, G1, T], F32, name="w1s")
+        a1 = keep.tile([P, 32], BF16, name="a1", align_bytes=64)
+        v1 = keep.tile([P, 32], BF16, name="v1", align_bytes=64)
+        t1 = keep.tile([P, 32], BF16, name="t1", align_bytes=64)
+        gain = keep.tile([P, 512], BF16, name="gain", align_bytes=64)
+        spread = keep.tile([P, G1 * 130], BF16, name="spread", align_bytes=64)
+        ident16 = keep.tile([P, P], BF16, name="ident16", align_bytes=64)
+        ident32 = keep.tile([P, P], F32, name="ident32", align_bytes=64)
+
+        for x in (a1, v1, t1):
+            nc.vector.memset(x[:], 1.0)
+        nc.vector.memset(gain[:], 0.0)
+        nc.gpsimd.memset(spread[:], 0.0)
+        make_identity(nc, ident16[:])
+        make_identity(nc, ident32[:])
+
+        nc.scalar.dma_start(out=w1s[:, 0:2, :], in_=scale_view[:, 0:2, :])
+        nc.scalar.dma_start(out=a1[:, 2:17], in_=a)
+        nc.scalar.dma_start(out=v1[:, 2:17], in_=v)
+        nc.scalar.dma_start(out=t1[:, 2:17], in_=t)
+        gz_view = gz.rearrange("(g h c) -> h g c", h=2, c=256)
+        for hb in range(2):
+            nc.scalar.dma_start(out=gain[hb:16:2, hb * 256 : (hb + 1) * 256], in_=gz_view[hb])
+        nc.scalar.dma_start(out=w1s[:, 2:G1, :], in_=scale_view[:, 2:G1, :])
+
+        raw1 = {}
+
+        def load_w1(g):
+            for j in range(2):
+                b = bytes_pool.tile([P, 2, H], U8, name="w1b", tag="w1b", align_bytes=64)
+                if g == 0:
+                    for s in range(2):
+                        nc.sync.dma_start(out=b[:, s : s + 1, :], in_=w1_view[g][:, 2 * j + s : 2 * j + s + 1, :])
+                else:
+                    nc.sync.dma_start(out=b[:], in_=w1_view[g][:, 2 * j : 2 * j + 2, :])
+                raw1[(g, j)] = b
+
+        raw2 = {}
+
+        def load_w2(w):
+            half, g = divmod(w, G2)
+            r = raw_pool.tile([P, T, HALF], BF16, name="w2raw", tag="w2raw", align_bytes=64)
+            nc.sync.dma_start(out=r[:], in_=w2_view[g][:, :, half * HALF : (half + 1) * HALF])
+            raw2[w] = r
+
+        wides = {}
+
+        def byte_cols(u, s, c0, c1):
+            g, half = divmod(u, 2)
+            return raw1[(g, s // 2)][:, s % 2, half * HALF + c0 : half * HALF + c1].bitcast(FP8)
+
+        def widen_vector(u):
+            g = u // 2
+            w = wide_pool.tile([P, T, HALF], BF16, name="wide", tag="wide", align_bytes=64)
+            wides[u] = w
+            nc.vector.tensor_scalar(
+                out=w[:, 3, HALF - V_COLS : HALF],
+                in0=byte_cols(u, 3, HALF - V_COLS, HALF),
+                scalar1=w1s[:, g, 3:4],
+                scalar2=None,
+                op0=ALU.mult,
+            )
+
+        def widen_scalar(u):
+            g = u // 2
+            w = wides[u]
+            for s in range(T):
+                c1 = HALF - V_COLS if s == 3 else HALF
+                nc.scalar.activation(out=w[:, s, 0:c1], in_=byte_cols(u, s, 0, c1), func=ACT.Copy, scale=w1s[:, g, s : s + 1])
+
+        def inter_out(tile_ap):
+            return tile_ap.rearrange("p (c i t) -> p c t i", i=4, t=T)
+
+        def inter_in(ap):
+            return ap.rearrange("p t (c i) -> p c t i", i=4)
+
+        def quantize(grp, pool, tag):
+            codes = pool.tile([P, Q], U32, name="c" + tag, tag="c" + tag, align_bytes=64)
+            scales = pool.tile([P, Q], U8, name="s" + tag, tag="s" + tag, align_bytes=64)
+            nc.vector.quantize_mx(out=codes[:].bitcast(FP8X4), scales=scales[:], in_=grp[:])
+            return codes, scales
+
+        load_w1(0)
+        load_w1(1)
+        load_w1(2)
+
+        nc.vector.tensor_copy(
+            out=spread[:].rearrange("p (g c) -> p g c", c=130)[:, :, 0:2],
+            in_=a1[:, 1:17].rearrange("p (g h) -> p g h", h=2),
+        )
+        vt_rows = keep.tile([P, 2, 16, 16], F32, name="vt_rows", align_bytes=64)
+        nc.vector.tensor_tensor(
+            out=vt_rows[:],
+            in0=v1[:, 1:17].unsqueeze(1).unsqueeze(3).to_broadcast([P, 2, 16, 16]),
+            in1=t1[:, 1:17].unsqueeze(1).unsqueeze(1).to_broadcast([P, 2, 16, 16]),
+            op=ALU.mult,
+        )
+        sel_ps = psum.tile([P, G1, TOK], BF16, name="sel_ps", tag="o0")
+        for g in range(G1):
+            nc.tensor.transpose(sel_ps[:, g, :], spread[:, 128 * g : 128 * (g + 1)], ident16[:])
+        vt_ps = psum.tile([P, T, TOK], F32, name="vt_ps", tag="o1")
+        vt_flat = vt_rows[:].rearrange("p h j k -> p (h j k)")
+        for s in range(T):
+            nc.tensor.transpose(vt_ps[:, s, :], vt_flat[:, s : 512 : 4], ident32[:])
+
+        widen_vector(0)
+        widen_vector(1)
+        sel = keep.tile([P, G1, TOK], BF16, name="sel", align_bytes=64)
+        nc.vector.tensor_copy(out=sel[:], in_=sel_ps[:])
+        vt = keep.tile([P, TOK, T], F32, name="vt", align_bytes=64)
+        nc.vector.tensor_copy(out=vt[:], in_=vt_ps[:].rearrange("p s n -> p n s"))
+
+        zgt = keep.tile([P, G1, TOK, T], BF16, name="zgt", align_bytes=64)
+        ga_tags = ["o2", "o3", "x0", "x1", "x2", "x3", "o0", "o1"]
+        ga_ps = []
+        for g in range(G1):
+            c = psum.tile([P, T, TOK], F32, name="ga" + str(g), tag=ga_tags[g])
+            for s in range(T):
+                nc.tensor.matmul(c[:, s, :], lhsT=gain[:, s : 512 : 4], rhs=sel[:, g, :], start=True, stop=True)
+            ga_ps.append(c)
+        for g in range(G1):
+            nc.vector.tensor_tensor(out=zgt[:, g], in0=ga_ps[g][:].rearrange("p s n -> p n s"), in1=vt[:], op=ALU.mult)
+        zq = keep.tile([P, G1 * TOK], U32, name="zq", align_bytes=64)
+        zs = keep.tile([P, G1 * TOK], U8, name="zs", align_bytes=64)
+        zflat = zgt[:].rearrange("p g n t -> p (g n t)")
+        for j in range(2):
+            nc.vector.quantize_mx(
+                out=zq[:, 512 * j : 512 * (j + 1)].bitcast(FP8X4),
+                scales=zs[:, 512 * j : 512 * (j + 1)],
+                in_=zflat[:, 2048 * j : 2048 * (j + 1)],
+            )
+
+        acc = [psum.tile([P, 512], F32, name="acc" + str(j), tag="x" + str(j)) for j in range(4)]
+
+        ghb = keep.tile([P, H], BF16, name="ghb", align_bytes=64)
+        for u in range(2 * G1):
+            g, half = divmod(u, 2)
+            if half == 0 and g + 3 < G1:
+                load_w1(g + 3)
+            if u == 10:
+                nc.sync.dma_start(out=ghb[:], in_=gh.partition_broadcast(128))
+                for w in range(6):
+                    load_w2(w)
+            widen_scalar(u)
+            if u + 2 < 2 * G1:
+                widen_vector(u + 2)
+            grp = []
+            for j in range(2):
+                gt = grp_pool.tile([P, Q * T], BF16, name="g" + str(j), tag="g" + str(j), align_bytes=64)
+                nc.vector.tensor_copy(out=inter_out(gt[:]), in_=inter_in(wides[u][:, :, j * Q : (j + 1) * Q]))
+                grp.append(gt)
+            for j in range(2):
+                codes, scales = quantize(grp[j], code_pool, "w1" + str(j))
+                nc.tensor.matmul_mx(
+                    out=acc[2 * half + j][:],
+                    lhsT=zq[:, 128 * g : 128 * (g + 1)].bitcast(FP8X4),
+                    lhsT_scale=zs[:, 128 * g : 128 * (g + 1)],
+                    rhs=codes[:].bitcast(FP8X4),
+                    rhs_scale=scales[:],
+                    start=(g == 0),
+                    stop=(g == G1 - 1),
+                )
+
+        h = keep.tile([P, H], BF16, name="h", align_bytes=64)
+        h_words = h[:].bitcast(F32)
+        hg = keep.tile([P, H], BF16, name="hg", align_bytes=64)
+        hg_grp = hg[:].rearrange("p (b x) -> p b x", b=2)
+        hq = keep.tile([P, G2 * TOK], U32, name="hq", align_bytes=64)
+        hs = keep.tile([P, G2 * TOK], U8, name="hs", align_bytes=64)
+        res = keep.tile([P, O], F32, name="res", align_bytes=64)
+        w2q = {}
+        acc2 = [psum.tile([P, 512], F32, name="acc2" + str(j), tag="o" + str(j)) for j in range(4)]
+
+        def prep_w2(w):
+            if w + 5 >= 6 and w + 5 < 2 * G2:
+                load_w2(w + 5)
+            gb = grp_pool.tile([P, Q * T], BF16, name="g2s", tag="g2s", align_bytes=64)
+            nc.scalar.copy(out=inter_out(gb[:]), in_=inter_in(raw2[w][:, :, Q:HALF]))
+            ga = grp_pool.tile([P, Q * T], BF16, name="g0", tag="g0", align_bytes=64)
+            nc.vector.tensor_copy(out=inter_out(ga[:]), in_=inter_in(raw2[w][:, :, 0:Q]))
+            qb = quantize(gb, keep, "w2b" + str(w))
+            qa = quantize(ga, keep, "w2a" + str(w))
+            w2q[w] = (qa, qb)
+
+        def multiply_w2(w):
+            half, g = divmod(w, G2)
+            for j in range(2):
+                codes, scales = w2q[w][j]
+                nc.tensor.matmul_mx(
+                    out=acc2[2 * half + j][:],
+                    lhsT=hq[:, 128 * g : 128 * (g + 1)].bitcast(FP8X4),
+                    lhsT_scale=hs[:, 128 * g : 128 * (g + 1)],
+                    rhs=codes[:].bitcast(FP8X4),
+                    rhs_scale=scales[:],
+                    start=(g == 0),
+                    stop=(g == G2 - 1),
+                )
+
+        def store(j):
+            nc.sync.dma_start(out=out[:, 512 * j : 512 * (j + 1)], in_=res[:, 512 * j : 512 * (j + 1)])
+
+        prep_w2(0)
+        for j in range(4):
+            nc.vector.scalar_tensor_tensor(
+                out=h[:, 512 * j : 512 * (j + 1)],
+                in0=acc[j][:],
+                scalar=0.0,
+                in1=ghb[:, 512 * j : 512 * (j + 1)],
+                op0=ALU.max,
+                op1=ALU.mult,
+            )
+        ht = []
+        for b in range(2):
+            hp = psum.tile([P, 2, 2, TOK], F32, name="ht" + str(b), tag="x" + str(b))
+            for g in range(2):
+                for e in range(2):
+                    base = 256 * (2 * b + g)
+                    nc.tensor.transpose(hp[:, g, e, :], h_words[:, base + e : base + 256 : 2], ident32[:])
+            ht.append(hp)
+        prep_w2(1)
+        for b in range(2):
+            nc.vector.tensor_copy(
+                out=hg_grp[:, b, :].bitcast(F32).rearrange("p (g n e) -> p g n e", g=2, e=2),
+                in_=ht[b][:].rearrange("p g e n -> p g n e"),
+            )
+        prep_w2(2)
+        for b in range(2):
+            nc.vector.quantize_mx(
+                out=hq[:, 256 * b : 256 * (b + 1)].bitcast(FP8X4),
+                scales=hs[:, 256 * b : 256 * (b + 1)],
+                in_=hg_grp[:, b, :],
+            )
+        for w in range(3):
+            multiply_w2(w)
+        for w in range(3, 8):
+            prep_w2(w)
+            multiply_w2(w)
+            if w == 5:
+                for j in range(2):
+                    nc.scalar.copy(out=res[:, 512 * j : 512 * (j + 1)], in_=acc2[j][:])
+                    store(j)
+        nc.scalar.copy(out=res[:, 1536:2048], in_=acc2[3][:])
+        nc.vector.tensor_copy(out=res[:, 1024:1536], in_=acc2[2][:])
+        store(3)
+        store(2)

@@ -21,10 +21,10 @@ O = 2048
 G1 = Z // 512
 G2 = H // 512
 HALF = 1024
-Q = 512
+S_COLS = [1024] + [576] * 7
+PE_COLS = [1024] + [0] * 7
+PE_AT = 11
 FLOPS = 2 * TOK * Z * H + 2 * TOK * H * O
-
-V_COLS = 256
 
 
 def tile_tensorfusionouterproducthead_w_kernel(tc, a, v, t, gz, w1_bytes, w1_scale, gh, w2, out):
@@ -33,9 +33,9 @@ def tile_tensorfusionouterproducthead_w_kernel(tc, a, v, t, gz, w1_bytes, w1_sca
         keep = ctx.enter_context(tc.tile_pool(name="keep", bufs=1))
         bytes_pool = ctx.enter_context(tc.tile_pool(name="bytes_pool", bufs=6))
         wide_pool = ctx.enter_context(tc.tile_pool(name="wide_pool", bufs=3))
-        grp_pool = ctx.enter_context(tc.tile_pool(name="grp_pool", bufs=3))
+        grp_pool = ctx.enter_context(tc.tile_pool(name="grp_pool", bufs=4))
         code_pool = ctx.enter_context(tc.tile_pool(name="code_pool", bufs=3))
-        raw_pool = ctx.enter_context(tc.tile_pool(name="raw_pool", bufs=6))
+        raw_pool = ctx.enter_context(tc.tile_pool(name="raw_pool", bufs=5))
         psum = ctx.enter_context(tc.psum_pool(name="psum", bufs=1))
         ctx.enter_context(tc.manual_schedule())
 
@@ -90,38 +90,40 @@ def tile_tensorfusionouterproducthead_w_kernel(tc, a, v, t, gz, w1_bytes, w1_sca
 
         wides = {}
 
-        def byte_cols(u, s, c0, c1):
-            g, half = divmod(u, 2)
-            return raw1[(g, s // 2)][:, s % 2, half * HALF + c0 : half * HALF + c1].bitcast(FP8)
+        def new_wide(g):
+            w = wide_pool.tile([P, T, H], BF16, name="wide", tag="wide", align_bytes=64)
+            wides[g] = w
 
-        def widen_vector(u):
-            g = u // 2
-            w = wide_pool.tile([P, T, HALF], BF16, name="wide", tag="wide", align_bytes=64)
-            wides[u] = w
+        def widen_vector(g, s):
             nc.vector.tensor_scalar(
-                out=w[:, 3, HALF - V_COLS : HALF],
-                in0=byte_cols(u, 3, HALF - V_COLS, HALF),
-                scalar1=w1s[:, g, 3:4],
+                out=wides[g][:, s, :],
+                in0=raw1[(g, s // 2)][:, s % 2, :].bitcast(FP8),
+                scalar1=w1s[:, g, s : s + 1],
                 scalar2=None,
                 op0=ALU.mult,
             )
 
-        def widen_scalar(u):
-            g = u // 2
-            w = wides[u]
-            for s in range(T):
-                c1 = HALF - V_COLS if s == 3 else HALF
-                nc.scalar.activation(out=w[:, s, 0:c1], in_=byte_cols(u, s, 0, c1), func=ACT.Copy, scale=w1s[:, g, s : s + 1])
+        def widen_scalar(g, s, c0, c1):
+            nc.scalar.activation(
+                out=wides[g][:, s, c0:c1],
+                in_=raw1[(g, s // 2)][:, s % 2, c0:c1].bitcast(FP8),
+                func=ACT.Copy,
+                scale=w1s[:, g, s : s + 1],
+            )
 
-        def inter_out(tile_ap):
-            return tile_ap.rearrange("p (c i t) -> p c t i", i=4, t=T)
+        def inter(copy, grp, src, c0, c1):
+            copy(
+                out=grp[:, T * c0 : T * c1].rearrange("p (c i t) -> p c t i", i=4, t=T),
+                in_=src.rearrange("p t (c i) -> p c t i", i=4),
+            )
 
-        def inter_in(ap):
-            return ap.rearrange("p t (c i) -> p c t i", i=4)
+        def new_grp():
+            grp = grp_pool.tile([P, HALF * T], BF16, name="grp", tag="grp", align_bytes=64)
+            return grp
 
-        def quantize(grp, pool, tag):
-            codes = pool.tile([P, Q], U32, name="c" + tag, tag="c" + tag, align_bytes=64)
-            scales = pool.tile([P, Q], U8, name="s" + tag, tag="s" + tag, align_bytes=64)
+        def quantize(grp, tag, bufs):
+            codes = code_pool.tile([P, HALF], U32, name="c" + tag, tag="c" + tag, bufs=bufs, align_bytes=64)
+            scales = code_pool.tile([P, HALF], U8, name="s" + tag, tag="s" + tag, bufs=bufs, align_bytes=64)
             nc.vector.quantize_mx(out=codes[:].bitcast(FP8X4), scales=scales[:], in_=grp[:])
             return codes, scales
 
@@ -129,6 +131,10 @@ def tile_tensorfusionouterproducthead_w_kernel(tc, a, v, t, gz, w1_bytes, w1_sca
         load_w1(1)
         load_w1(2)
 
+        new_wide(0)
+        new_wide(1)
+        widen_vector(0, 0)
+        widen_vector(0, 2)
         nc.vector.tensor_copy(
             out=spread[:].rearrange("p (g c) -> p g c", c=130)[:, :, 0:2],
             in_=a1[:, 1:17].rearrange("p (g h) -> p g h", h=2),
@@ -147,9 +153,10 @@ def tile_tensorfusionouterproducthead_w_kernel(tc, a, v, t, gz, w1_bytes, w1_sca
         vt_flat = vt_rows[:].rearrange("p h j k -> p (h j k)")
         for s in range(T):
             nc.tensor.transpose(vt_ps[:, s, :], vt_flat[:, s : 512 : 4], ident32[:])
+        widen_vector(1, 0)
+        widen_scalar(0, 1, 0, H)
+        widen_scalar(0, 3, 0, H)
 
-        widen_vector(0)
-        widen_vector(1)
         sel = keep.tile([P, G1, TOK], BF16, name="sel", align_bytes=64)
         nc.vector.tensor_copy(out=sel[:], in_=sel_ps[:])
         vt = keep.tile([P, TOK, T], F32, name="vt", align_bytes=64)
@@ -167,44 +174,82 @@ def tile_tensorfusionouterproducthead_w_kernel(tc, a, v, t, gz, w1_bytes, w1_sca
             nc.vector.tensor_tensor(out=zgt[:, g], in0=ga_ps[g][:].rearrange("p s n -> p n s"), in1=vt[:], op=ALU.mult)
         zq = keep.tile([P, G1 * TOK], U32, name="zq", align_bytes=64)
         zs = keep.tile([P, G1 * TOK], U8, name="zs", align_bytes=64)
-        zflat = zgt[:].rearrange("p g n t -> p (g n t)")
-        for j in range(2):
-            nc.vector.quantize_mx(
-                out=zq[:, 512 * j : 512 * (j + 1)].bitcast(FP8X4),
-                scales=zs[:, 512 * j : 512 * (j + 1)],
-                in_=zflat[:, 2048 * j : 2048 * (j + 1)],
-            )
+        nc.vector.quantize_mx(out=zq[:].bitcast(FP8X4), scales=zs[:], in_=zgt[:].rearrange("p g n t -> p (g n t)"))
 
         acc = [psum.tile([P, 512], F32, name="acc" + str(j), tag="x" + str(j)) for j in range(4)]
 
         ghb = keep.tile([P, H], BF16, name="ghb", align_bytes=64)
-        for u in range(2 * G1):
+        grps = {}
+
+        def quantize_multiply_w1(u):
             g, half = divmod(u, 2)
-            if half == 0 and g + 3 < G1:
-                load_w1(g + 3)
-            if u == 10:
-                nc.sync.dma_start(out=ghb[:], in_=gh.partition_broadcast(128))
-                for w in range(6):
-                    load_w2(w)
-            widen_scalar(u)
-            if u + 2 < 2 * G1:
-                widen_vector(u + 2)
-            grp = []
+            codes, scales = quantize(grps.pop(u), "w1", 3)
             for j in range(2):
-                gt = grp_pool.tile([P, Q * T], BF16, name="g" + str(j), tag="g" + str(j), align_bytes=64)
-                nc.vector.tensor_copy(out=inter_out(gt[:]), in_=inter_in(wides[u][:, :, j * Q : (j + 1) * Q]))
-                grp.append(gt)
-            for j in range(2):
-                codes, scales = quantize(grp[j], code_pool, "w1" + str(j))
                 nc.tensor.matmul_mx(
                     out=acc[2 * half + j][:],
                     lhsT=zq[:, 128 * g : 128 * (g + 1)].bitcast(FP8X4),
                     lhsT_scale=zs[:, 128 * g : 128 * (g + 1)],
-                    rhs=codes[:].bitcast(FP8X4),
-                    rhs_scale=scales[:],
+                    rhs=codes[:, 512 * j : 512 * (j + 1)].bitcast(FP8X4),
+                    rhs_scale=scales[:, 512 * j : 512 * (j + 1)],
                     start=(g == 0),
                     stop=(g == G1 - 1),
                 )
+
+        w2g = {}
+        w2q = {}
+
+        def inter_w2(w):
+            grp = new_grp()
+            w2g[w] = grp
+            c = HALF - S_COLS[w]
+            d = c + PE_COLS[w]
+            for c0 in range(c, d, 256):
+                nc.scalar.copy(out=grp[:, T * c0 : T * (c0 + 256)], in_=banks[(w, c0)][:].rearrange("p j x -> p (j x)"))
+            if d < HALF:
+                inter(nc.scalar.copy, grp, raw2[w][:, :, d:HALF], d, HALF)
+            if c > 0:
+                inter(nc.vector.tensor_copy, grp, raw2[w][:, :, 0:c], 0, c)
+
+        banks = {}
+
+        def tensor_inter_w2(w):
+            c = HALF - S_COLS[w]
+            for k, c0 in enumerate(range(c, c + PE_COLS[w], 256)):
+                bank = psum.tile([P, 2, 512], BF16, name="bank" + str(k), tag="o" + str(k))
+                for j in range(2):
+                    n0 = c0 + 128 * j
+                    nc.tensor.matmul(bank[:, j, :], lhsT=ident16[:], rhs=raw2[w][:, :, n0 : n0 + 128].rearrange("p t n -> p n t"), start=True, stop=True)
+                banks[(w, c0)] = bank
+
+        for g in range(G1):
+            if g + 3 < G1:
+                load_w1(g + 3)
+            if g == 4:
+                nc.sync.dma_start(out=ghb[:], in_=gh.partition_broadcast(128))
+                for w in range(5):
+                    load_w2(w)
+            if g > 1:
+                new_wide(g)
+            if g > 0:
+                first = 1 if g == 1 else 0
+                if g < 5:
+                    for s in range(first, T):
+                        widen_scalar(g, s, 0, H)
+                else:
+                    for c0 in (0, HALF):
+                        for s in range(T):
+                            widen_scalar(g, s, c0, c0 + HALF)
+            for half in range(2):
+                u = 2 * g + half
+                grps[u] = new_grp()
+                inter(nc.vector.tensor_copy, grps[u], wides[g][:, :, half * HALF : (half + 1) * HALF], 0, HALF)
+                if u > 0:
+                    quantize_multiply_w1(u - 1)
+                if u == PE_AT:
+                    tensor_inter_w2(0)
+        inter_w2(0)
+        quantize_multiply_w1(2 * G1 - 1)
+        inter_w2(1)
 
         h = keep.tile([P, H], BF16, name="h", align_bytes=64)
         h_words = h[:].bitcast(F32)
@@ -213,38 +258,32 @@ def tile_tensorfusionouterproducthead_w_kernel(tc, a, v, t, gz, w1_bytes, w1_sca
         hq = keep.tile([P, G2 * TOK], U32, name="hq", align_bytes=64)
         hs = keep.tile([P, G2 * TOK], U8, name="hs", align_bytes=64)
         res = keep.tile([P, O], F32, name="res", align_bytes=64)
-        w2q = {}
-        acc2 = [psum.tile([P, 512], F32, name="acc2" + str(j), tag="o" + str(j)) for j in range(4)]
-
-        def prep_w2(w):
-            if w + 5 >= 6 and w + 5 < 2 * G2:
-                load_w2(w + 5)
-            gb = grp_pool.tile([P, Q * T], BF16, name="g2s", tag="g2s", align_bytes=64)
-            nc.scalar.copy(out=inter_out(gb[:]), in_=inter_in(raw2[w][:, :, Q:HALF]))
-            ga = grp_pool.tile([P, Q * T], BF16, name="g0", tag="g0", align_bytes=64)
-            nc.vector.tensor_copy(out=inter_out(ga[:]), in_=inter_in(raw2[w][:, :, 0:Q]))
-            qb = quantize(gb, keep, "w2b" + str(w))
-            qa = quantize(ga, keep, "w2a" + str(w))
-            w2q[w] = (qa, qb)
+        acc2 = {}
+        def quantize_w2(w):
+            w2q[w] = quantize(w2g[w], "w2", 4)
 
         def multiply_w2(w):
             half, g = divmod(w, G2)
+            codes, scales = w2q[w]
             for j in range(2):
-                codes, scales = w2q[w][j]
+                if g == 0:
+                    acc2[2 * half + j] = psum.tile([P, 512], F32, name="acc2" + str(2 * half + j), tag="o" + str(2 * half + j))
                 nc.tensor.matmul_mx(
                     out=acc2[2 * half + j][:],
                     lhsT=hq[:, 128 * g : 128 * (g + 1)].bitcast(FP8X4),
                     lhsT_scale=hs[:, 128 * g : 128 * (g + 1)],
-                    rhs=codes[:].bitcast(FP8X4),
-                    rhs_scale=scales[:],
+                    rhs=codes[:, 512 * j : 512 * (j + 1)].bitcast(FP8X4),
+                    rhs_scale=scales[:, 512 * j : 512 * (j + 1)],
                     start=(g == 0),
                     stop=(g == G2 - 1),
                 )
 
+        def finish(copy, j, c0, c1):
+            copy(out=res[:, 512 * j + c0 : 512 * j + c1], in_=acc2[j][:, c0:c1])
+
         def store(j):
             nc.sync.dma_start(out=out[:, 512 * j : 512 * (j + 1)], in_=res[:, 512 * j : 512 * (j + 1)])
 
-        prep_w2(0)
         for j in range(4):
             nc.vector.scalar_tensor_tensor(
                 out=h[:, 512 * j : 512 * (j + 1)],
@@ -254,6 +293,7 @@ def tile_tensorfusionouterproducthead_w_kernel(tc, a, v, t, gz, w1_bytes, w1_sca
                 op0=ALU.max,
                 op1=ALU.mult,
             )
+        quantize_w2(0)
         ht = []
         for b in range(2):
             hp = psum.tile([P, 2, 2, TOK], F32, name="ht" + str(b), tag="x" + str(b))
@@ -262,29 +302,37 @@ def tile_tensorfusionouterproducthead_w_kernel(tc, a, v, t, gz, w1_bytes, w1_sca
                     base = 256 * (2 * b + g)
                     nc.tensor.transpose(hp[:, g, e, :], h_words[:, base + e : base + 256 : 2], ident32[:])
             ht.append(hp)
-        prep_w2(1)
+        load_w2(5)
+        inter_w2(2)
+        quantize_w2(1)
         for b in range(2):
-            nc.vector.tensor_copy(
+            nc.scalar.copy(
                 out=hg_grp[:, b, :].bitcast(F32).rearrange("p (g n e) -> p g n e", g=2, e=2),
                 in_=ht[b][:].rearrange("p g e n -> p g n e"),
             )
-        prep_w2(2)
+        load_w2(6)
+        inter_w2(3)
         for b in range(2):
             nc.vector.quantize_mx(
                 out=hq[:, 256 * b : 256 * (b + 1)].bitcast(FP8X4),
                 scales=hs[:, 256 * b : 256 * (b + 1)],
                 in_=hg_grp[:, b, :],
             )
-        for w in range(3):
-            multiply_w2(w)
-        for w in range(3, 8):
-            prep_w2(w)
-            multiply_w2(w)
-            if w == 5:
-                for j in range(2):
-                    nc.scalar.copy(out=res[:, 512 * j : 512 * (j + 1)], in_=acc2[j][:])
-                    store(j)
-        nc.scalar.copy(out=res[:, 1536:2048], in_=acc2[3][:])
-        nc.vector.tensor_copy(out=res[:, 1024:1536], in_=acc2[2][:])
-        store(3)
+        quantize_w2(2)
+        multiply_w2(0)
+        multiply_w2(1)
+        multiply_w2(2)
+        load_w2(7)
+        for w in range(4, 8):
+            inter_w2(w)
+            quantize_w2(w - 1)
+            multiply_w2(w - 1)
+        for j in range(2):
+            finish(nc.scalar.copy, j, 0, 512)
+            store(j)
+        quantize_w2(7)
+        multiply_w2(7)
+        finish(nc.scalar.copy, 2, 0, 512)
         store(2)
+        finish(nc.vector.tensor_copy, 3, 0, 512)
+        store(3)

@@ -21,8 +21,9 @@ O = 2048
 G1 = Z // 512
 G2 = H // 512
 HALF = 1024
-S_COLS = [1024] + [576] * 7
-PE_COLS = [1024] + [0] * 7
+S_COLS = [1024] + [640] * 6 + [512]
+PE_COLS = [1024, 0, 256] + [0] * 5
+G_COLS = 640
 PE_AT = 11
 FLOPS = 2 * TOK * Z * H + 2 * TOK * H * O
 
@@ -52,6 +53,9 @@ def tile_tensorfusionouterproducthead_w_kernel(tc, a, v, t, gz, w1_bytes, w1_sca
         ident16 = keep.tile([P, P], BF16, name="ident16", align_bytes=64)
         ident32 = keep.tile([P, P], F32, name="ident32", align_bytes=64)
 
+        warm = keep.tile([P, 1], F32, name="warm")
+        nc.vector.memset(warm[:], 0.0)
+        nc.scalar.activation(out=warm[:], in_=warm[:], func=ACT.Copy)
         for x in (a1, v1, t1):
             nc.vector.memset(x[:], 1.0)
         nc.vector.memset(gain[:], 0.0)
@@ -59,14 +63,13 @@ def tile_tensorfusionouterproducthead_w_kernel(tc, a, v, t, gz, w1_bytes, w1_sca
         make_identity(nc, ident16[:])
         make_identity(nc, ident32[:])
 
-        nc.scalar.dma_start(out=w1s[:, 0:2, :], in_=scale_view[:, 0:2, :])
+        nc.sync.dma_start(out=w1s[:, 0:2, :], in_=scale_view[:, 0:2, :])
         nc.scalar.dma_start(out=a1[:, 2:17], in_=a)
         nc.scalar.dma_start(out=v1[:, 2:17], in_=v)
         nc.scalar.dma_start(out=t1[:, 2:17], in_=t)
         gz_view = gz.rearrange("(g h c) -> h g c", h=2, c=256)
         for hb in range(2):
-            nc.scalar.dma_start(out=gain[hb:16:2, hb * 256 : (hb + 1) * 256], in_=gz_view[hb])
-        nc.scalar.dma_start(out=w1s[:, 2:G1, :], in_=scale_view[:, 2:G1, :])
+            nc.gpsimd.dma_start(out=gain[hb:16:2, hb * 256 : (hb + 1) * 256], in_=gz_view[hb])
 
         raw1 = {}
 
@@ -129,6 +132,7 @@ def tile_tensorfusionouterproducthead_w_kernel(tc, a, v, t, gz, w1_bytes, w1_sca
 
         load_w1(0)
         load_w1(1)
+        nc.sync.dma_start(out=w1s[:, 2:G1, :], in_=scale_view[:, 2:G1, :])
         load_w1(2)
 
         new_wide(0)
@@ -178,8 +182,18 @@ def tile_tensorfusionouterproducthead_w_kernel(tc, a, v, t, gz, w1_bytes, w1_sca
 
         acc = [psum.tile([P, 512], F32, name="acc" + str(j), tag="x" + str(j)) for j in range(4)]
 
+        grps = {0: new_grp()}
+        for c0 in range(HALF - G_COLS, HALF, 128):
+            nc.gpsimd.tensor_scalar(
+                out=grps[0][:, T * c0 : T * (c0 + 128)].rearrange("p (n t) -> p n t", t=T),
+                in0=wides[0][:, :, c0 : c0 + 128].rearrange("p t n -> p n t"),
+                scalar1=1.0,
+                scalar2=0.0,
+                op0=ALU.mult,
+                op1=ALU.add,
+            )
+
         ghb = keep.tile([P, H], BF16, name="ghb", align_bytes=64)
-        grps = {}
 
         def quantize_multiply_w1(u):
             g, half = divmod(u, 2)
@@ -203,10 +217,10 @@ def tile_tensorfusionouterproducthead_w_kernel(tc, a, v, t, gz, w1_bytes, w1_sca
             w2g[w] = grp
             c = HALF - S_COLS[w]
             d = c + PE_COLS[w]
-            for c0 in range(c, d, 256):
-                nc.scalar.copy(out=grp[:, T * c0 : T * (c0 + 256)], in_=banks[(w, c0)][:].rearrange("p j x -> p (j x)"))
             if d < HALF:
                 inter(nc.scalar.copy, grp, raw2[w][:, :, d:HALF], d, HALF)
+            for c0 in range(c, d, 256):
+                nc.scalar.copy(out=grp[:, T * c0 : T * (c0 + 256)], in_=banks[(w, c0)][:].rearrange("p j x -> p (j x)"))
             if c > 0:
                 inter(nc.vector.tensor_copy, grp, raw2[w][:, :, 0:c], 0, c)
 
@@ -241,14 +255,19 @@ def tile_tensorfusionouterproducthead_w_kernel(tc, a, v, t, gz, w1_bytes, w1_sca
                             widen_scalar(g, s, c0, c0 + HALF)
             for half in range(2):
                 u = 2 * g + half
-                grps[u] = new_grp()
-                inter(nc.vector.tensor_copy, grps[u], wides[g][:, :, half * HALF : (half + 1) * HALF], 0, HALF)
+                c1 = HALF
+                if u > 0:
+                    grps[u] = new_grp()
+                else:
+                    c1 = HALF - G_COLS
+                inter(nc.vector.tensor_copy, grps[u], wides[g][:, :, half * HALF : half * HALF + c1], 0, c1)
                 if u > 0:
                     quantize_multiply_w1(u - 1)
                 if u == PE_AT:
                     tensor_inter_w2(0)
         inter_w2(0)
         quantize_multiply_w1(2 * G1 - 1)
+        tensor_inter_w2(2)
         inter_w2(1)
 
         h = keep.tile([P, H], BF16, name="h", align_bytes=64)
@@ -330,7 +349,12 @@ def tile_tensorfusionouterproducthead_w_kernel(tc, a, v, t, gz, w1_bytes, w1_sca
         for j in range(2):
             finish(nc.scalar.copy, j, 0, 512)
             store(j)
-        quantize_w2(7)
+        codes = code_pool.tile([P, HALF], U32, name="cw2", tag="cw2", bufs=4, align_bytes=64)
+        scales = code_pool.tile([P, HALF], U8, name="sw2", tag="sw2", bufs=4, align_bytes=64)
+        for j in range(2):
+            c = slice(512 * j, 512 * (j + 1))
+            nc.vector.quantize_mx(out=codes[:, c].bitcast(FP8X4), scales=scales[:, c], in_=w2g[7][:, 2048 * j : 2048 * (j + 1)])
+        w2q[7] = (codes, scales)
         multiply_w2(7)
         finish(nc.scalar.copy, 2, 0, 512)
         store(2)

@@ -9,23 +9,36 @@ U32 = mybir.dt.uint32
 U8 = mybir.dt.uint8
 FP8 = mybir.dt.float8_e4m3fn
 FP8X4 = mybir.dt.float8_e4m3fn_x4
-ALU = mybir.AluOpType
-ACT = mybir.ActivationFunctionType
+MULT = mybir.AluOpType.mult
+ADD = mybir.AluOpType.add
+MAX = mybir.AluOpType.max
+COPY = mybir.ActivationFunctionType.Copy
 
 P = 128
-T = 4
-TOK = 128
-Z = 4096
+SLOTS = 4
+PASS = P * SLOTS
+TOKENS = 128
+FACTOR = 16
+Z = FACTOR * FACTOR * FACTOR
 H = 2048
 O = 2048
-G1 = Z // 512
-G2 = H // 512
+PASSES1 = Z // PASS
+PASSES2 = H // PASS
 HALF = 1024
-S_COLS = [1024] + [640] * 6 + [512]
-PE_COLS = [1024, 0, 256] + [0] * 5
-G_COLS = 640
-PE_AT = 11
-FLOPS = 2 * TOK * Z * H + 2 * TOK * H * O
+BANK = 512
+PIECE = 128
+PAIR = 2
+INNER = FACTOR * FACTOR
+
+FLOPS = 2 * TOKENS * Z * H + 2 * TOKENS * H * O
+
+SCALAR_COLUMNS = [1024, 640, 640, 640, 640, 640, 640, 448]
+TENSOR_COLUMNS = [1024, 0, 256, 0, 0, 0, 0, 0]
+GPSIMD_COLUMNS_W1 = 640
+GPSIMD_COLUMNS_W2 = 384
+GPSIMD_HALF_PASS_W2 = 2
+TENSOR_TURN = 11
+FINE_PASS = 5
 
 
 def tile_tensorfusionouterproducthead_w_kernel(tc, a, v, t, gz, w1_bytes, w1_scale, gh, w2, out):
@@ -34,28 +47,32 @@ def tile_tensorfusionouterproducthead_w_kernel(tc, a, v, t, gz, w1_bytes, w1_sca
         keep = ctx.enter_context(tc.tile_pool(name="keep", bufs=1))
         bytes_pool = ctx.enter_context(tc.tile_pool(name="bytes_pool", bufs=6))
         wide_pool = ctx.enter_context(tc.tile_pool(name="wide_pool", bufs=3))
-        grp_pool = ctx.enter_context(tc.tile_pool(name="grp_pool", bufs=4))
+        grouped_pool = ctx.enter_context(tc.tile_pool(name="grouped_pool", bufs=4))
         code_pool = ctx.enter_context(tc.tile_pool(name="code_pool", bufs=3))
         raw_pool = ctx.enter_context(tc.tile_pool(name="raw_pool", bufs=5))
         psum = ctx.enter_context(tc.psum_pool(name="psum", bufs=1))
         ctx.enter_context(tc.manual_schedule())
 
-        w1_view = w1_bytes.rearrange("(g p t) n -> g p t n", p=P, t=T)
-        w2_view = w2.rearrange("(g p t) n -> g p t n", p=P, t=T)
-        scale_view = w1_scale.rearrange("(g p t) o -> p g (t o)", p=P, t=T)
 
-        w1s = keep.tile([P, G1, T], F32, name="w1s")
+        w1_view = w1_bytes.rearrange("(g p t) n -> g p t n", p=P, t=SLOTS)
+        w2_view = w2.rearrange("(g p t) n -> g p t n", p=P, t=SLOTS)
+        scale_view = w1_scale.rearrange("(g p t) o -> p g (t o)", p=P, t=SLOTS)
+        gz_view = gz.rearrange("(g h c) -> h g c", h=PAIR, c=INNER)
+
+        w1s = keep.tile([P, PASSES1, SLOTS], F32, name="w1s")
         a1 = keep.tile([P, 32], BF16, name="a1", align_bytes=64)
         v1 = keep.tile([P, 32], BF16, name="v1", align_bytes=64)
         t1 = keep.tile([P, 32], BF16, name="t1", align_bytes=64)
-        gain = keep.tile([P, 512], BF16, name="gain", align_bytes=64)
-        spread = keep.tile([P, G1 * 130], BF16, name="spread", align_bytes=64)
+        gain = keep.tile([P, PASS], BF16, name="gain", align_bytes=64)
+        spread_step = P + PAIR
+        spread = keep.tile([P, PASSES1 * spread_step], BF16, name="spread", align_bytes=64)
         ident16 = keep.tile([P, P], BF16, name="ident16", align_bytes=64)
         ident32 = keep.tile([P, P], F32, name="ident32", align_bytes=64)
+        ghb = keep.tile([P, H], BF16, name="ghb", align_bytes=64)
 
-        warm = keep.tile([P, 1], F32, name="warm")
-        nc.vector.memset(warm[:], 0.0)
-        nc.scalar.activation(out=warm[:], in_=warm[:], func=ACT.Copy)
+        table = keep.tile([P, 1], F32, name="table")
+        nc.vector.memset(table[:], 0.0)
+        nc.scalar.activation(out=table[:], in_=table[:], func=COPY)
         for x in (a1, v1, t1):
             nc.vector.memset(x[:], 1.0)
         nc.vector.memset(gain[:], 0.0)
@@ -64,299 +81,299 @@ def tile_tensorfusionouterproducthead_w_kernel(tc, a, v, t, gz, w1_bytes, w1_sca
         make_identity(nc, ident32[:])
 
         nc.sync.dma_start(out=w1s[:, 0:2, :], in_=scale_view[:, 0:2, :])
-        nc.scalar.dma_start(out=a1[:, 2:17], in_=a)
-        nc.scalar.dma_start(out=v1[:, 2:17], in_=v)
-        nc.scalar.dma_start(out=t1[:, 2:17], in_=t)
-        gz_view = gz.rearrange("(g h c) -> h g c", h=2, c=256)
-        for hb in range(2):
-            nc.gpsimd.dma_start(out=gain[hb:16:2, hb * 256 : (hb + 1) * 256], in_=gz_view[hb])
+        for tile, source in ((a1, a), (v1, v), (t1, t)):
+            nc.scalar.dma_start(out=tile[:, 2 : 1 + FACTOR], in_=source)
+        for e in range(PAIR):
+            nc.gpsimd.dma_start(out=gain[e:FACTOR:PAIR, e * INNER : (e + 1) * INNER], in_=gz_view[e])
 
-        raw1 = {}
+        w1_raw = {}
+        w2_raw = {}
 
         def load_w1(g):
-            for j in range(2):
-                b = bytes_pool.tile([P, 2, H], U8, name="w1b", tag="w1b", align_bytes=64)
-                if g == 0:
+            for pair in range(2):
+                raw = bytes_pool.tile([P, 2, H], U8, name="w1_bytes_tile", tag="w1_bytes_tile", align_bytes=64)
+                w1_raw[(g, pair)] = raw
+            if g == 0:
+                for c0 in (0, HALF):
                     for s in range(2):
-                        nc.sync.dma_start(out=b[:, s : s + 1, :], in_=w1_view[g][:, 2 * j + s : 2 * j + s + 1, :])
-                else:
-                    nc.sync.dma_start(out=b[:], in_=w1_view[g][:, 2 * j : 2 * j + 2, :])
-                raw1[(g, j)] = b
-
-        raw2 = {}
+                        piece = slice(c0, c0 + HALF)
+                        nc.sync.dma_start(out=w1_raw[(0, 0)][:, s : s + 1, piece], in_=w1_view[0][:, s : s + 1, piece])
+            else:
+                nc.sync.dma_start(out=w1_raw[(g, 0)][:], in_=w1_view[g][:, 0:2, :])
+            nc.sync.dma_start(out=w1_raw[(g, 1)][:], in_=w1_view[g][:, 2:4, :])
 
         def load_w2(w):
-            half, g = divmod(w, G2)
-            r = raw_pool.tile([P, T, HALF], BF16, name="w2raw", tag="w2raw", align_bytes=64)
-            nc.sync.dma_start(out=r[:], in_=w2_view[g][:, :, half * HALF : (half + 1) * HALF])
-            raw2[w] = r
+            half, g = divmod(w, PASSES2)
+            raw = raw_pool.tile([P, SLOTS, HALF], BF16, name="w2_raw", tag="w2_raw", align_bytes=64)
+            nc.sync.dma_start(out=raw[:], in_=w2_view[g][:, :, half * HALF : (half + 1) * HALF])
+            w2_raw[w] = raw
 
-        wides = {}
+        wide = {}
 
         def new_wide(g):
-            w = wide_pool.tile([P, T, H], BF16, name="wide", tag="wide", align_bytes=64)
-            wides[g] = w
+            tile = wide_pool.tile([P, SLOTS, H], BF16, name="wide", tag="wide", align_bytes=64)
+            wide[g] = tile
 
-        def widen_vector(g, s):
+        def byte_values(g, s, c0, c1):
+            return w1_raw[(g, s // 2)][:, s % 2, c0:c1].bitcast(FP8)
+
+        def widen_vector(g, s, c0, c1):
             nc.vector.tensor_scalar(
-                out=wides[g][:, s, :],
-                in0=raw1[(g, s // 2)][:, s % 2, :].bitcast(FP8),
-                scalar1=w1s[:, g, s : s + 1],
-                scalar2=None,
-                op0=ALU.mult,
+                out=wide[g][:, s, c0:c1], in0=byte_values(g, s, c0, c1), scalar1=w1s[:, g, s : s + 1], scalar2=None, op0=MULT
             )
 
         def widen_scalar(g, s, c0, c1):
-            nc.scalar.activation(
-                out=wides[g][:, s, c0:c1],
-                in_=raw1[(g, s // 2)][:, s % 2, c0:c1].bitcast(FP8),
-                func=ACT.Copy,
-                scale=w1s[:, g, s : s + 1],
-            )
+            nc.scalar.activation(out=wide[g][:, s, c0:c1], in_=byte_values(g, s, c0, c1), func=COPY, scale=w1s[:, g, s : s + 1])
 
-        def inter(copy, grp, src, c0, c1):
+        def new_grouped():
+            tile = grouped_pool.tile([P, HALF * SLOTS], BF16, name="grouped", tag="grouped", align_bytes=64)
+            return tile
+
+        def interleave(copy, grouped, source, c0, c1):
             copy(
-                out=grp[:, T * c0 : T * c1].rearrange("p (c i t) -> p c t i", i=4, t=T),
-                in_=src.rearrange("p t (c i) -> p c t i", i=4),
+                out=grouped[:, SLOTS * c0 : SLOTS * c1].rearrange("p (c i t) -> p c t i", i=4, t=SLOTS),
+                in_=source.rearrange("p t (c i) -> p c t i", i=4),
             )
 
-        def new_grp():
-            grp = grp_pool.tile([P, HALF * T], BF16, name="grp", tag="grp", align_bytes=64)
-            return grp
+        def interleave_gpsimd(grouped, source, c0, one):
+            nc.gpsimd.tensor_scalar(
+                out=grouped[:, SLOTS * c0 : SLOTS * (c0 + PIECE)].rearrange("p (n t) -> p n t", t=SLOTS),
+                in0=source[:, :, c0 : c0 + PIECE].rearrange("p t n -> p n t"),
+                scalar1=one,
+                scalar2=0.0,
+                op0=MULT,
+                op1=ADD,
+            )
 
-        def quantize(grp, tag, bufs):
-            codes = code_pool.tile([P, HALF], U32, name="c" + tag, tag="c" + tag, bufs=bufs, align_bytes=64)
-            scales = code_pool.tile([P, HALF], U8, name="s" + tag, tag="s" + tag, bufs=bufs, align_bytes=64)
-            nc.vector.quantize_mx(out=codes[:].bitcast(FP8X4), scales=scales[:], in_=grp[:])
+        def new_codes(tag, bufs):
+            codes = code_pool.tile([P, HALF], U32, name=tag + "_codes", tag=tag + "_codes", bufs=bufs, align_bytes=64)
+            scales = code_pool.tile([P, HALF], U8, name=tag + "_scales", tag=tag + "_scales", bufs=bufs, align_bytes=64)
             return codes, scales
+
+        def quantize(codes, scales, grouped, c0, c1):
+            nc.vector.quantize_mx(
+                out=codes[:, c0:c1].bitcast(FP8X4), scales=scales[:, c0:c1], in_=grouped[:, SLOTS * c0 : SLOTS * c1]
+            )
+
+        def multiply(bank, left, g, right, half_bank, passes):
+            rows = slice(TOKENS * g, TOKENS * (g + 1))
+            cols = slice(BANK * half_bank, BANK * (half_bank + 1))
+            nc.tensor.matmul_mx(
+                out=bank[:],
+                lhsT=left[0][:, rows].bitcast(FP8X4),
+                lhsT_scale=left[1][:, rows],
+                rhs=right[0][:, cols].bitcast(FP8X4),
+                rhs_scale=right[1][:, cols],
+                start=(g == 0),
+                stop=(g == passes - 1),
+            )
 
         load_w1(0)
         load_w1(1)
-        nc.sync.dma_start(out=w1s[:, 2:G1, :], in_=scale_view[:, 2:G1, :])
+        nc.sync.dma_start(out=w1s[:, 2:PASSES1, :], in_=scale_view[:, 2:PASSES1, :])
         load_w1(2)
 
         new_wide(0)
         new_wide(1)
-        widen_vector(0, 0)
-        widen_vector(0, 2)
+        widen_vector(0, 0, 0, HALF)
+        widen_vector(0, 0, HALF, H)
         nc.vector.tensor_copy(
-            out=spread[:].rearrange("p (g c) -> p g c", c=130)[:, :, 0:2],
-            in_=a1[:, 1:17].rearrange("p (g h) -> p g h", h=2),
+            out=spread[:].rearrange("p (g c) -> p g c", c=spread_step)[:, :, 0:PAIR],
+            in_=a1[:, 1 : 1 + FACTOR].rearrange("p (g e) -> p g e", e=PAIR),
         )
-        vt_rows = keep.tile([P, 2, 16, 16], F32, name="vt_rows", align_bytes=64)
+        vt_shape = [P, PAIR, FACTOR, FACTOR]
+        vt_rows = keep.tile(vt_shape, F32, name="vt_rows", align_bytes=64)
         nc.vector.tensor_tensor(
             out=vt_rows[:],
-            in0=v1[:, 1:17].unsqueeze(1).unsqueeze(3).to_broadcast([P, 2, 16, 16]),
-            in1=t1[:, 1:17].unsqueeze(1).unsqueeze(1).to_broadcast([P, 2, 16, 16]),
-            op=ALU.mult,
+            in0=v1[:, 1 : 1 + FACTOR].unsqueeze(1).unsqueeze(3).to_broadcast(vt_shape),
+            in1=t1[:, 1 : 1 + FACTOR].unsqueeze(1).unsqueeze(1).to_broadcast(vt_shape),
+            op=MULT,
         )
-        sel_ps = psum.tile([P, G1, TOK], BF16, name="sel_ps", tag="o0")
-        for g in range(G1):
-            nc.tensor.transpose(sel_ps[:, g, :], spread[:, 128 * g : 128 * (g + 1)], ident16[:])
-        vt_ps = psum.tile([P, T, TOK], F32, name="vt_ps", tag="o1")
-        vt_flat = vt_rows[:].rearrange("p h j k -> p (h j k)")
-        for s in range(T):
-            nc.tensor.transpose(vt_ps[:, s, :], vt_flat[:, s : 512 : 4], ident32[:])
-        widen_vector(1, 0)
-        widen_scalar(0, 1, 0, H)
+        only_bank = psum.tile([P, PASSES1, TOKENS], BF16, name="only_bank", tag="o0")
+        for g in range(PASSES1):
+            nc.tensor.transpose(only_bank[:, g, :], spread[:, P * g : P * (g + 1)], ident16[:])
+        vt_bank = psum.tile([P, SLOTS, TOKENS], F32, name="vt_bank", tag="o1")
+        vt_flat = vt_rows[:].rearrange("p e j k -> p (e j k)")
+        for s in range(SLOTS):
+            nc.tensor.transpose(vt_bank[:, s, :], vt_flat[:, s:PASS:SLOTS], ident32[:])
+        widen_vector(0, 2, 0, H)
+        widen_vector(1, 0, 0, H)
+        widen_scalar(0, 1, 0, HALF)
+        widen_scalar(0, 1, HALF, H)
         widen_scalar(0, 3, 0, H)
+        only = keep.tile([P, PASSES1, TOKENS], BF16, name="only", align_bytes=64)
+        nc.vector.tensor_copy(out=only[:], in_=only_bank[:])
+        vt = keep.tile([P, TOKENS, SLOTS], F32, name="vt", align_bytes=64)
+        nc.vector.tensor_copy(out=vt[:], in_=vt_bank[:].rearrange("p s n -> p n s"))
 
-        sel = keep.tile([P, G1, TOK], BF16, name="sel", align_bytes=64)
-        nc.vector.tensor_copy(out=sel[:], in_=sel_ps[:])
-        vt = keep.tile([P, TOK, T], F32, name="vt", align_bytes=64)
-        nc.vector.tensor_copy(out=vt[:], in_=vt_ps[:].rearrange("p s n -> p n s"))
+        zg = keep.tile([P, PASSES1, TOKENS, SLOTS], BF16, name="zg", align_bytes=64)
+        a_gz = []
+        for g, tag in enumerate(("o2", "o3", "x0", "x1", "x2", "x3", "o0", "o1")):
+            bank = psum.tile([P, SLOTS, TOKENS], F32, name="a_gz" + str(g), tag=tag)
+            for s in range(SLOTS):
+                nc.tensor.matmul(bank[:, s, :], lhsT=gain[:, s:PASS:SLOTS], rhs=only[:, g, :], start=True, stop=True)
+            a_gz.append(bank)
+        for g in range(PASSES1):
+            nc.vector.tensor_tensor(out=zg[:, g], in0=a_gz[g][:].rearrange("p s n -> p n s"), in1=vt[:], op=MULT)
+        zg_codes = keep.tile([P, PASSES1 * TOKENS], U32, name="zg_codes", align_bytes=64)
+        zg_scales = keep.tile([P, PASSES1 * TOKENS], U8, name="zg_scales", align_bytes=64)
+        nc.vector.quantize_mx(
+            out=zg_codes[:].bitcast(FP8X4), scales=zg_scales[:], in_=zg[:].rearrange("p g n t -> p (g n t)")
+        )
 
-        zgt = keep.tile([P, G1, TOK, T], BF16, name="zgt", align_bytes=64)
-        ga_tags = ["o2", "o3", "x0", "x1", "x2", "x3", "o0", "o1"]
-        ga_ps = []
-        for g in range(G1):
-            c = psum.tile([P, T, TOK], F32, name="ga" + str(g), tag=ga_tags[g])
-            for s in range(T):
-                nc.tensor.matmul(c[:, s, :], lhsT=gain[:, s : 512 : 4], rhs=sel[:, g, :], start=True, stop=True)
-            ga_ps.append(c)
-        for g in range(G1):
-            nc.vector.tensor_tensor(out=zgt[:, g], in0=ga_ps[g][:].rearrange("p s n -> p n s"), in1=vt[:], op=ALU.mult)
-        zq = keep.tile([P, G1 * TOK], U32, name="zq", align_bytes=64)
-        zs = keep.tile([P, G1 * TOK], U8, name="zs", align_bytes=64)
-        nc.vector.quantize_mx(out=zq[:].bitcast(FP8X4), scales=zs[:], in_=zgt[:].rearrange("p g n t -> p (g n t)"))
+        sums1 = [psum.tile([P, BANK], F32, name="sums1_" + str(j), tag="x" + str(j)) for j in range(H // BANK)]
+        w1_grouped = {0: new_grouped()}
+        for c0 in range(HALF - GPSIMD_COLUMNS_W1, HALF, PIECE):
+            interleave_gpsimd(w1_grouped[0], wide[0], c0, 1.0)
 
-        acc = [psum.tile([P, 512], F32, name="acc" + str(j), tag="x" + str(j)) for j in range(4)]
-
-        grps = {0: new_grp()}
-        for c0 in range(HALF - G_COLS, HALF, 128):
-            nc.gpsimd.tensor_scalar(
-                out=grps[0][:, T * c0 : T * (c0 + 128)].rearrange("p (n t) -> p n t", t=T),
-                in0=wides[0][:, :, c0 : c0 + 128].rearrange("p t n -> p n t"),
-                scalar1=1.0,
-                scalar2=0.0,
-                op0=ALU.mult,
-                op1=ALU.add,
-            )
-
-        ghb = keep.tile([P, H], BF16, name="ghb", align_bytes=64)
+        def interleave_w1(u):
+            g, half = divmod(u, 2)
+            c1 = HALF
+            if u > 0:
+                w1_grouped[u] = new_grouped()
+            else:
+                c1 = HALF - GPSIMD_COLUMNS_W1
+            interleave(nc.vector.tensor_copy, w1_grouped[u], wide[g][:, :, half * HALF : half * HALF + c1], 0, c1)
 
         def quantize_multiply_w1(u):
             g, half = divmod(u, 2)
-            codes, scales = quantize(grps.pop(u), "w1", 3)
+            right = new_codes("w1", 3)
+            quantize(right[0], right[1], w1_grouped[u], 0, HALF)
             for j in range(2):
-                nc.tensor.matmul_mx(
-                    out=acc[2 * half + j][:],
-                    lhsT=zq[:, 128 * g : 128 * (g + 1)].bitcast(FP8X4),
-                    lhsT_scale=zs[:, 128 * g : 128 * (g + 1)],
-                    rhs=codes[:, 512 * j : 512 * (j + 1)].bitcast(FP8X4),
-                    rhs_scale=scales[:, 512 * j : 512 * (j + 1)],
-                    start=(g == 0),
-                    stop=(g == G1 - 1),
-                )
+                multiply(sums1[2 * half + j], (zg_codes, zg_scales), g, right, j, PASSES1)
 
-        w2g = {}
-        w2q = {}
+        w2_grouped = {}
+        w2_banks = {}
+        start_flag = keep.tile([P, 1], F32, name="start_flag")
 
-        def inter_w2(w):
-            grp = new_grp()
-            w2g[w] = grp
-            c = HALF - S_COLS[w]
-            d = c + PE_COLS[w]
-            if d < HALF:
-                inter(nc.scalar.copy, grp, raw2[w][:, :, d:HALF], d, HALF)
-            for c0 in range(c, d, 256):
-                nc.scalar.copy(out=grp[:, T * c0 : T * (c0 + 256)], in_=banks[(w, c0)][:].rearrange("p j x -> p (j x)"))
-            if c > 0:
-                inter(nc.vector.tensor_copy, grp, raw2[w][:, :, 0:c], 0, c)
-
-        banks = {}
-
-        def tensor_inter_w2(w):
-            c = HALF - S_COLS[w]
-            for k, c0 in enumerate(range(c, c + PE_COLS[w], 256)):
-                bank = psum.tile([P, 2, 512], BF16, name="bank" + str(k), tag="o" + str(k))
+        def interleave_w2_tensor(w):
+            first = HALF - SCALAR_COLUMNS[w]
+            for b, c0 in enumerate(range(first, first + TENSOR_COLUMNS[w], 2 * PIECE)):
+                bank = psum.tile([P, 2, PIECE * SLOTS], BF16, name="w2_bank" + str(b), tag="o" + str(b))
                 for j in range(2):
-                    n0 = c0 + 128 * j
-                    nc.tensor.matmul(bank[:, j, :], lhsT=ident16[:], rhs=raw2[w][:, :, n0 : n0 + 128].rearrange("p t n -> p n t"), start=True, stop=True)
-                banks[(w, c0)] = bank
+                    n0 = c0 + PIECE * j
+                    moving = w2_raw[w][:, :, n0 : n0 + PIECE].rearrange("p t n -> p n t")
+                    nc.tensor.matmul(bank[:, j, :], lhsT=ident16[:], rhs=moving, start=True, stop=True)
+                w2_banks[(w, c0)] = bank
 
-        for g in range(G1):
-            if g + 3 < G1:
+        def interleave_w2(w):
+            grouped = new_grouped()
+            w2_grouped[w] = grouped
+            raw = w2_raw[w]
+            first = HALF - SCALAR_COLUMNS[w]
+            direct = first + TENSOR_COLUMNS[w]
+            if direct < HALF:
+                interleave(nc.scalar.copy, grouped, raw[:, :, direct:HALF], direct, HALF)
+            for c0 in range(first, direct, 2 * PIECE):
+                bank = w2_banks[(w, c0)]
+                nc.scalar.copy(out=grouped[:, SLOTS * c0 : SLOTS * (c0 + 2 * PIECE)], in_=bank[:].rearrange("p j x -> p (j x)"))
+            begin = 0
+            if w == GPSIMD_HALF_PASS_W2:
+                begin = GPSIMD_COLUMNS_W2
+                for c0 in range(0, begin, PIECE):
+                    interleave_gpsimd(grouped, raw, c0, start_flag[:])
+            if begin < first:
+                interleave(nc.vector.tensor_copy, grouped, raw[:, :, begin:first], begin, first)
+
+        for g in range(PASSES1):
+            if g + 3 < PASSES1:
                 load_w1(g + 3)
             if g == 4:
-                nc.sync.dma_start(out=ghb[:], in_=gh.partition_broadcast(128))
+                nc.sync.dma_start(out=ghb[:], in_=gh.partition_broadcast(P))
                 for w in range(5):
                     load_w2(w)
             if g > 1:
                 new_wide(g)
             if g > 0:
-                first = 1 if g == 1 else 0
-                if g < 5:
-                    for s in range(first, T):
-                        widen_scalar(g, s, 0, H)
-                else:
-                    for c0 in (0, HALF):
-                        for s in range(T):
-                            widen_scalar(g, s, c0, c0 + HALF)
+                widths = (H,) if g < FINE_PASS else (HALF, HALF)
+                for b, width in enumerate(widths):
+                    for s in range(1 if g == 1 else 0, SLOTS):
+                        widen_scalar(g, s, b * width, (b + 1) * width)
             for half in range(2):
                 u = 2 * g + half
-                c1 = HALF
-                if u > 0:
-                    grps[u] = new_grp()
-                else:
-                    c1 = HALF - G_COLS
-                inter(nc.vector.tensor_copy, grps[u], wides[g][:, :, half * HALF : half * HALF + c1], 0, c1)
+                interleave_w1(u)
                 if u > 0:
                     quantize_multiply_w1(u - 1)
-                if u == PE_AT:
-                    tensor_inter_w2(0)
-        inter_w2(0)
-        quantize_multiply_w1(2 * G1 - 1)
-        tensor_inter_w2(2)
-        inter_w2(1)
+                if u == TENSOR_TURN:
+                    interleave_w2_tensor(0)
+        interleave_w2(0)
+        quantize_multiply_w1(2 * PASSES1 - 1)
+        interleave_w2_tensor(2)
+        interleave_w2(1)
 
         h = keep.tile([P, H], BF16, name="h", align_bytes=64)
-        h_words = h[:].bitcast(F32)
-        hg = keep.tile([P, H], BF16, name="hg", align_bytes=64)
-        hg_grp = hg[:].rearrange("p (b x) -> p b x", b=2)
-        hq = keep.tile([P, G2 * TOK], U32, name="hq", align_bytes=64)
-        hs = keep.tile([P, G2 * TOK], U8, name="hs", align_bytes=64)
-        res = keep.tile([P, O], F32, name="res", align_bytes=64)
-        acc2 = {}
+        h_grouped = keep.tile([P, PASSES2, TOKENS * SLOTS], BF16, name="h_grouped", align_bytes=64)
+        h_codes = keep.tile([P, PASSES2 * TOKENS], U32, name="h_codes", align_bytes=64)
+        h_scales = keep.tile([P, PASSES2 * TOKENS], U8, name="h_scales", align_bytes=64)
+        result = keep.tile([P, O], F32, name="result", align_bytes=64)
+        sums2 = {}
+        w2_codes = {}
+
         def quantize_w2(w):
-            w2q[w] = quantize(w2g[w], "w2", 4)
+            w2_codes[w] = new_codes("w2", 4)
+            quantize(w2_codes[w][0], w2_codes[w][1], w2_grouped[w], 0, HALF)
 
         def multiply_w2(w):
-            half, g = divmod(w, G2)
-            codes, scales = w2q[w]
+            half, g = divmod(w, PASSES2)
             for j in range(2):
+                b = 2 * half + j
                 if g == 0:
-                    acc2[2 * half + j] = psum.tile([P, 512], F32, name="acc2" + str(2 * half + j), tag="o" + str(2 * half + j))
-                nc.tensor.matmul_mx(
-                    out=acc2[2 * half + j][:],
-                    lhsT=hq[:, 128 * g : 128 * (g + 1)].bitcast(FP8X4),
-                    lhsT_scale=hs[:, 128 * g : 128 * (g + 1)],
-                    rhs=codes[:, 512 * j : 512 * (j + 1)].bitcast(FP8X4),
-                    rhs_scale=scales[:, 512 * j : 512 * (j + 1)],
-                    start=(g == 0),
-                    stop=(g == G2 - 1),
-                )
+                    sums2[b] = psum.tile([P, BANK], F32, name="sums2_" + str(b), tag="o" + str(b))
+                multiply(sums2[b], (h_codes, h_scales), g, w2_codes[w], j, PASSES2)
 
-        def finish(copy, j, c0, c1):
-            copy(out=res[:, 512 * j + c0 : 512 * j + c1], in_=acc2[j][:, c0:c1])
+        def store(copy, b):
+            cols = slice(BANK * b, BANK * (b + 1))
+            copy(out=result[:, cols], in_=sums2[b][:])
+            nc.sync.dma_start(out=out[:, cols], in_=result[:, cols])
 
-        def store(j):
-            nc.sync.dma_start(out=out[:, 512 * j : 512 * (j + 1)], in_=res[:, 512 * j : 512 * (j + 1)])
-
-        for j in range(4):
+        nc.vector.memset(start_flag[:], 1.0)
+        for j in range(H // BANK):
+            cols = slice(BANK * j, BANK * (j + 1))
             nc.vector.scalar_tensor_tensor(
-                out=h[:, 512 * j : 512 * (j + 1)],
-                in0=acc[j][:],
-                scalar=0.0,
-                in1=ghb[:, 512 * j : 512 * (j + 1)],
-                op0=ALU.max,
-                op1=ALU.mult,
+                out=h[:, cols], in0=sums1[j][:], scalar=0.0, in1=ghb[:, cols], op0=MAX, op1=MULT
             )
         quantize_w2(0)
-        ht = []
+        h_words = h[:].bitcast(F32)
+        h_banks = []
         for b in range(2):
-            hp = psum.tile([P, 2, 2, TOK], F32, name="ht" + str(b), tag="x" + str(b))
+            bank = psum.tile([P, 2, 2, TOKENS], F32, name="h_bank" + str(b), tag="x" + str(b))
             for g in range(2):
                 for e in range(2):
                     base = 256 * (2 * b + g)
-                    nc.tensor.transpose(hp[:, g, e, :], h_words[:, base + e : base + 256 : 2], ident32[:])
-            ht.append(hp)
+                    nc.tensor.transpose(bank[:, g, e, :], h_words[:, base + e : base + 256 : 2], ident32[:])
+            h_banks.append(bank)
         load_w2(5)
-        inter_w2(2)
+        interleave_w2(2)
         quantize_w2(1)
         for b in range(2):
+            words = h_grouped[:, 2 * b : 2 * b + 2, :].rearrange("p g x -> p (g x)").bitcast(F32)
             nc.scalar.copy(
-                out=hg_grp[:, b, :].bitcast(F32).rearrange("p (g n e) -> p g n e", g=2, e=2),
-                in_=ht[b][:].rearrange("p g e n -> p g n e"),
+                out=words.rearrange("p (g n e) -> p g n e", g=2, e=2), in_=h_banks[b][:].rearrange("p g e n -> p g n e")
             )
         load_w2(6)
-        inter_w2(3)
+        interleave_w2(3)
         for b in range(2):
+            cols = slice(2 * TOKENS * b, 2 * TOKENS * (b + 1))
             nc.vector.quantize_mx(
-                out=hq[:, 256 * b : 256 * (b + 1)].bitcast(FP8X4),
-                scales=hs[:, 256 * b : 256 * (b + 1)],
-                in_=hg_grp[:, b, :],
+                out=h_codes[:, cols].bitcast(FP8X4),
+                scales=h_scales[:, cols],
+                in_=h_grouped[:, 2 * b : 2 * b + 2, :].rearrange("p g x -> p (g x)"),
             )
         quantize_w2(2)
-        multiply_w2(0)
-        multiply_w2(1)
-        multiply_w2(2)
+
+        for w in range(3):
+            multiply_w2(w)
         load_w2(7)
-        for w in range(4, 8):
-            inter_w2(w)
+        for w in range(4, 2 * PASSES2):
+            interleave_w2(w)
             quantize_w2(w - 1)
             multiply_w2(w - 1)
-        for j in range(2):
-            finish(nc.scalar.copy, j, 0, 512)
-            store(j)
-        codes = code_pool.tile([P, HALF], U32, name="cw2", tag="cw2", bufs=4, align_bytes=64)
-        scales = code_pool.tile([P, HALF], U8, name="sw2", tag="sw2", bufs=4, align_bytes=64)
-        for j in range(2):
-            c = slice(512 * j, 512 * (j + 1))
-            nc.vector.quantize_mx(out=codes[:, c].bitcast(FP8X4), scales=scales[:, c], in_=w2g[7][:, 2048 * j : 2048 * (j + 1)])
-        w2q[7] = (codes, scales)
-        multiply_w2(7)
-        finish(nc.scalar.copy, 2, 0, 512)
-        store(2)
-        finish(nc.vector.tensor_copy, 3, 0, 512)
-        store(3)
+        store(nc.scalar.copy, 0)
+        store(nc.scalar.copy, 1)
+        last = 2 * PASSES2 - 1
+        w2_codes[last] = new_codes("w2", 4)
+        for c0 in (0, BANK):
+            quantize(w2_codes[last][0], w2_codes[last][1], w2_grouped[last], c0, c0 + BANK)
+        multiply_w2(last)
+        store(nc.scalar.copy, 2)
+        store(nc.vector.tensor_copy, 3)

@@ -131,8 +131,8 @@ def tile_tensorfusionouterproducthead_w_kernel(tc, a, v, t, gz, w1_bytes, w1_sca
 
         def interleave(copy, grouped, source, c0, c1):
             copy(
-                out=grouped[:, SLOTS * c0 : SLOTS * c1].rearrange("p (c i t) -> p c t i", i=4, t=SLOTS),
-                in_=source.rearrange("p t (c i) -> p c t i", i=4),
+                out=grouped[:, SLOTS * c0 : SLOTS * c1].rearrange("p (c i t) -> p c t i", i=8, t=SLOTS),
+                in_=source.rearrange("p t (c i) -> p c t i", i=8),
             )
 
         def interleave_gpsimd(grouped, source, c0, one):

from contextlib import ExitStack

import concourse.mybir as mybir
from concourse.masks import make_identity

F32 = mybir.dt.float32
BF16 = mybir.dt.bfloat16
U32 = mybir.dt.uint32
U8 = mybir.dt.uint8
FP8 = mybir.dt.float8_e4m3fn
FP8X4 = mybir.dt.float8_e4m3fn_x4
MULT = mybir.AluOpType.mult
ADD = mybir.AluOpType.add
MAX = mybir.AluOpType.max
COPY = mybir.ActivationFunctionType.Copy

P = 128
SLOTS = 4
PASS = P * SLOTS
TOKENS = 128
FACTOR = 16
Z = FACTOR * FACTOR * FACTOR
H = 2048
O = 2048
PASSES1 = Z // PASS
PASSES2 = H // PASS
HALF = 1024
BANK = 512
PIECE = 128
PAIR = 2
INNER = FACTOR * FACTOR

FLOPS = 2 * TOKENS * Z * H + 2 * TOKENS * H * O

SCALAR_COLUMNS = [1024, 640, 640, 640, 640, 640, 640, 448]
TENSOR_COLUMNS = [1024, 0, 256, 0, 0, 0, 0, 0]
GPSIMD_COLUMNS_W1 = 640
GPSIMD_COLUMNS_W2 = 384
GPSIMD_HALF_PASS_W2 = 2
TENSOR_TURN = 11
FINE_PASS = 5


def tile_tensorfusionouterproducthead_w_kernel(tc, a, v, t, gz, w1_bytes, w1_scale, gh, w2, out):
    nc = tc.nc
    with ExitStack() as ctx:
        keep = ctx.enter_context(tc.tile_pool(name="keep", bufs=1))
        bytes_pool = ctx.enter_context(tc.tile_pool(name="bytes_pool", bufs=6))
        wide_pool = ctx.enter_context(tc.tile_pool(name="wide_pool", bufs=3))
        grouped_pool = ctx.enter_context(tc.tile_pool(name="grouped_pool", bufs=4))
        code_pool = ctx.enter_context(tc.tile_pool(name="code_pool", bufs=3))
        raw_pool = ctx.enter_context(tc.tile_pool(name="raw_pool", bufs=5))
        psum = ctx.enter_context(tc.psum_pool(name="psum", bufs=1))
        ctx.enter_context(tc.manual_schedule())


        w1_view = w1_bytes.rearrange("(g p t) n -> g p t n", p=P, t=SLOTS)
        w2_view = w2.rearrange("(g p t) n -> g p t n", p=P, t=SLOTS)
        scale_view = w1_scale.rearrange("(g p t) o -> p g (t o)", p=P, t=SLOTS)
        gz_view = gz.rearrange("(g h c) -> h g c", h=PAIR, c=INNER)

        w1s = keep.tile([P, PASSES1, SLOTS], F32, name="w1s")
        a1 = keep.tile([P, 32], BF16, name="a1", align_bytes=64)
        v1 = keep.tile([P, 32], BF16, name="v1", align_bytes=64)
        t1 = keep.tile([P, 32], BF16, name="t1", align_bytes=64)
        gain = keep.tile([P, PASS], BF16, name="gain", align_bytes=64)
        spread_step = P + PAIR
        spread = keep.tile([P, PASSES1 * spread_step], BF16, name="spread", align_bytes=64)
        ident16 = keep.tile([P, P], BF16, name="ident16", align_bytes=64)
        ident32 = keep.tile([P, P], F32, name="ident32", align_bytes=64)
        ghb = keep.tile([P, H], BF16, name="ghb", align_bytes=64)

        table = keep.tile([P, 1], F32, name="table")
        nc.vector.memset(table[:], 0.0)
        nc.scalar.activation(out=table[:], in_=table[:], func=COPY)
        for x in (a1, v1, t1):
            nc.vector.memset(x[:], 1.0)
        nc.vector.memset(gain[:], 0.0)
        nc.gpsimd.memset(spread[:], 0.0)
        make_identity(nc, ident16[:])
        make_identity(nc, ident32[:])

        nc.sync.dma_start(out=w1s[:, 0:2, :], in_=scale_view[:, 0:2, :])
        for tile, source in ((a1, a), (v1, v), (t1, t)):
            nc.scalar.dma_start(out=tile[:, 2 : 1 + FACTOR], in_=source)
        for e in range(PAIR):
            nc.gpsimd.dma_start(out=gain[e:FACTOR:PAIR, e * INNER : (e + 1) * INNER], in_=gz_view[e])

        w1_raw = {}
        w2_raw = {}

        def load_w1(g):
            for pair in range(2):
                raw = bytes_pool.tile([P, 2, H], U8, name="w1_bytes_tile", tag="w1_bytes_tile", align_bytes=64)
                w1_raw[(g, pair)] = raw
            if g == 0:
                for c0 in (0, HALF):
                    for s in range(2):
                        piece = slice(c0, c0 + HALF)
                        nc.sync.dma_start(out=w1_raw[(0, 0)][:, s : s + 1, piece], in_=w1_view[0][:, s : s + 1, piece])
            else:
                nc.sync.dma_start(out=w1_raw[(g, 0)][:], in_=w1_view[g][:, 0:2, :])
            nc.sync.dma_start(out=w1_raw[(g, 1)][:], in_=w1_view[g][:, 2:4, :])

        def load_w2(w):
            half, g = divmod(w, PASSES2)
            raw = raw_pool.tile([P, SLOTS, HALF], BF16, name="w2_raw", tag="w2_raw", align_bytes=64)
            nc.sync.dma_start(out=raw[:], in_=w2_view[g][:, :, half * HALF : (half + 1) * HALF])
            w2_raw[w] = raw

        wide = {}

        def new_wide(g):
            tile = wide_pool.tile([P, SLOTS, H], BF16, name="wide", tag="wide", align_bytes=64)
            wide[g] = tile

        def byte_values(g, s, c0, c1):
            return w1_raw[(g, s // 2)][:, s % 2, c0:c1].bitcast(FP8)

        def widen_vector(g, s, c0, c1):
            nc.vector.tensor_scalar(
                out=wide[g][:, s, c0:c1], in0=byte_values(g, s, c0, c1), scalar1=w1s[:, g, s : s + 1], scalar2=None, op0=MULT
            )

        def widen_scalar(g, s, c0, c1):
            nc.scalar.activation(out=wide[g][:, s, c0:c1], in_=byte_values(g, s, c0, c1), func=COPY, scale=w1s[:, g, s : s + 1])

        def new_grouped():
            tile = grouped_pool.tile([P, HALF * SLOTS], BF16, name="grouped", tag="grouped", align_bytes=64)
            return tile

        def interleave(copy, grouped, source, c0, c1):
            copy(
                out=grouped[:, SLOTS * c0 : SLOTS * c1].rearrange("p (c i t) -> p c t i", i=8, t=SLOTS),
                in_=source.rearrange("p t (c i) -> p c t i", i=8),
            )

        def interleave_gpsimd(grouped, source, c0, one):
            nc.gpsimd.tensor_scalar(
                out=grouped[:, SLOTS * c0 : SLOTS * (c0 + PIECE)].rearrange("p (n t) -> p n t", t=SLOTS),
                in0=source[:, :, c0 : c0 + PIECE].rearrange("p t n -> p n t"),
                scalar1=one,
                scalar2=0.0,
                op0=MULT,
                op1=ADD,
            )

        def new_codes(tag, bufs):
            codes = code_pool.tile([P, HALF], U32, name=tag + "_codes", tag=tag + "_codes", bufs=bufs, align_bytes=64)
            scales = code_pool.tile([P, HALF], U8, name=tag + "_scales", tag=tag + "_scales", bufs=bufs, align_bytes=64)
            return codes, scales

        def quantize(codes, scales, grouped, c0, c1):
            nc.vector.quantize_mx(
                out=codes[:, c0:c1].bitcast(FP8X4), scales=scales[:, c0:c1], in_=grouped[:, SLOTS * c0 : SLOTS * c1]
            )

        def multiply(bank, left, g, right, half_bank, passes):
            rows = slice(TOKENS * g, TOKENS * (g + 1))
            cols = slice(BANK * half_bank, BANK * (half_bank + 1))
            nc.tensor.matmul_mx(
                out=bank[:],
                lhsT=left[0][:, rows].bitcast(FP8X4),
                lhsT_scale=left[1][:, rows],
                rhs=right[0][:, cols].bitcast(FP8X4),
                rhs_scale=right[1][:, cols],
                start=(g == 0),
                stop=(g == passes - 1),
            )

        load_w1(0)
        load_w1(1)
        nc.sync.dma_start(out=w1s[:, 2:PASSES1, :], in_=scale_view[:, 2:PASSES1, :])
        load_w1(2)

        new_wide(0)
        new_wide(1)
        widen_vector(0, 0, 0, HALF)
        widen_vector(0, 0, HALF, H)
        nc.vector.tensor_copy(
            out=spread[:].rearrange("p (g c) -> p g c", c=spread_step)[:, :, 0:PAIR],
            in_=a1[:, 1 : 1 + FACTOR].rearrange("p (g e) -> p g e", e=PAIR),
        )
        vt_shape = [P, PAIR, FACTOR, FACTOR]
        vt_rows = keep.tile(vt_shape, F32, name="vt_rows", align_bytes=64)
        nc.vector.tensor_tensor(
            out=vt_rows[:],
            in0=v1[:, 1 : 1 + FACTOR].unsqueeze(1).unsqueeze(3).to_broadcast(vt_shape),
            in1=t1[:, 1 : 1 + FACTOR].unsqueeze(1).unsqueeze(1).to_broadcast(vt_shape),
            op=MULT,
        )
        only_bank = psum.tile([P, PASSES1, TOKENS], BF16, name="only_bank", tag="o0")
        for g in range(PASSES1):
            nc.tensor.transpose(only_bank[:, g, :], spread[:, P * g : P * (g + 1)], ident16[:])
        vt_bank = psum.tile([P, SLOTS, TOKENS], F32, name="vt_bank", tag="o1")
        vt_flat = vt_rows[:].rearrange("p e j k -> p (e j k)")
        for s in range(SLOTS):
            nc.tensor.transpose(vt_bank[:, s, :], vt_flat[:, s:PASS:SLOTS], ident32[:])
        widen_vector(0, 2, 0, H)
        widen_vector(1, 0, 0, H)
        widen_scalar(0, 1, 0, HALF)
        widen_scalar(0, 1, HALF, H)
        widen_scalar(0, 3, 0, H)
        only = keep.tile([P, PASSES1, TOKENS], BF16, name="only", align_bytes=64)
        nc.vector.tensor_copy(out=only[:], in_=only_bank[:])
        vt = keep.tile([P, TOKENS, SLOTS], F32, name="vt", align_bytes=64)
        nc.vector.tensor_copy(out=vt[:], in_=vt_bank[:].rearrange("p s n -> p n s"))

        zg = keep.tile([P, PASSES1, TOKENS, SLOTS], BF16, name="zg", align_bytes=64)
        a_gz = []
        for g, tag in enumerate(("o2", "o3", "x0", "x1", "x2", "x3", "o0", "o1")):
            bank = psum.tile([P, SLOTS, TOKENS], F32, name="a_gz" + str(g), tag=tag)
            for s in range(SLOTS):
                nc.tensor.matmul(bank[:, s, :], lhsT=gain[:, s:PASS:SLOTS], rhs=only[:, g, :], start=True, stop=True)
            a_gz.append(bank)
        for g in range(PASSES1):
            nc.vector.tensor_tensor(out=zg[:, g], in0=a_gz[g][:].rearrange("p s n -> p n s"), in1=vt[:], op=MULT)
        zg_codes = keep.tile([P, PASSES1 * TOKENS], U32, name="zg_codes", align_bytes=64)
        zg_scales = keep.tile([P, PASSES1 * TOKENS], U8, name="zg_scales", align_bytes=64)
        nc.vector.quantize_mx(
            out=zg_codes[:].bitcast(FP8X4), scales=zg_scales[:], in_=zg[:].rearrange("p g n t -> p (g n t)")
        )

        sums1 = [psum.tile([P, BANK], F32, name="sums1_" + str(j), tag="x" + str(j)) for j in range(H // BANK)]
        w1_grouped = {0: new_grouped()}
        for c0 in range(HALF - GPSIMD_COLUMNS_W1, HALF, PIECE):
            interleave_gpsimd(w1_grouped[0], wide[0], c0, 1.0)

        def interleave_w1(u):
            g, half = divmod(u, 2)
            c1 = HALF
            if u > 0:
                w1_grouped[u] = new_grouped()
            else:
                c1 = HALF - GPSIMD_COLUMNS_W1
            interleave(nc.vector.tensor_copy, w1_grouped[u], wide[g][:, :, half * HALF : half * HALF + c1], 0, c1)

        def quantize_multiply_w1(u):
            g, half = divmod(u, 2)
            right = new_codes("w1", 3)
            quantize(right[0], right[1], w1_grouped[u], 0, HALF)
            for j in range(2):
                multiply(sums1[2 * half + j], (zg_codes, zg_scales), g, right, j, PASSES1)

        w2_grouped = {}
        w2_banks = {}
        start_flag = keep.tile([P, 1], F32, name="start_flag")

        def interleave_w2_tensor(w):
            first = HALF - SCALAR_COLUMNS[w]
            for b, c0 in enumerate(range(first, first + TENSOR_COLUMNS[w], 2 * PIECE)):
                bank = psum.tile([P, 2, PIECE * SLOTS], BF16, name="w2_bank" + str(b), tag="o" + str(b))
                for j in range(2):
                    n0 = c0 + PIECE * j
                    moving = w2_raw[w][:, :, n0 : n0 + PIECE].rearrange("p t n -> p n t")
                    nc.tensor.matmul(bank[:, j, :], lhsT=ident16[:], rhs=moving, start=True, stop=True)
                w2_banks[(w, c0)] = bank

        def interleave_w2(w):
            grouped = new_grouped()
            w2_grouped[w] = grouped
            raw = w2_raw[w]
            first = HALF - SCALAR_COLUMNS[w]
            direct = first + TENSOR_COLUMNS[w]
            if direct < HALF:
                interleave(nc.scalar.copy, grouped, raw[:, :, direct:HALF], direct, HALF)
            for c0 in range(first, direct, 2 * PIECE):
                bank = w2_banks[(w, c0)]
                nc.scalar.copy(out=grouped[:, SLOTS * c0 : SLOTS * (c0 + 2 * PIECE)], in_=bank[:].rearrange("p j x -> p (j x)"))
            begin = 0
            if w == GPSIMD_HALF_PASS_W2:
                begin = GPSIMD_COLUMNS_W2
                for c0 in range(0, begin, PIECE):
                    interleave_gpsimd(grouped, raw, c0, start_flag[:])
            if begin < first:
                interleave(nc.vector.tensor_copy, grouped, raw[:, :, begin:first], begin, first)

        for g in range(PASSES1):
            if g + 3 < PASSES1:
                load_w1(g + 3)
            if g == 4:
                nc.sync.dma_start(out=ghb[:], in_=gh.partition_broadcast(P))
                for w in range(5):
                    load_w2(w)
            if g > 1:
                new_wide(g)
            if g > 0:
                widths = (H,) if g < FINE_PASS else (HALF, HALF)
                for b, width in enumerate(widths):
                    for s in range(1 if g == 1 else 0, SLOTS):
                        widen_scalar(g, s, b * width, (b + 1) * width)
            for half in range(2):
                u = 2 * g + half
                interleave_w1(u)
                if u > 0:
                    quantize_multiply_w1(u - 1)
                if u == TENSOR_TURN:
                    interleave_w2_tensor(0)
        interleave_w2(0)
        quantize_multiply_w1(2 * PASSES1 - 1)
        interleave_w2_tensor(2)
        interleave_w2(1)

        h = keep.tile([P, H], BF16, name="h", align_bytes=64)
        h_grouped = keep.tile([P, PASSES2, TOKENS * SLOTS], BF16, name="h_grouped", align_bytes=64)
        h_codes = keep.tile([P, PASSES2 * TOKENS], U32, name="h_codes", align_bytes=64)
        h_scales = keep.tile([P, PASSES2 * TOKENS], U8, name="h_scales", align_bytes=64)
        result = keep.tile([P, O], F32, name="result", align_bytes=64)
        sums2 = {}
        w2_codes = {}

        def quantize_w2(w):
            w2_codes[w] = new_codes("w2", 4)
            quantize(w2_codes[w][0], w2_codes[w][1], w2_grouped[w], 0, HALF)

        def multiply_w2(w):
            half, g = divmod(w, PASSES2)
            for j in range(2):
                b = 2 * half + j
                if g == 0:
                    sums2[b] = psum.tile([P, BANK], F32, name="sums2_" + str(b), tag="o" + str(b))
                multiply(sums2[b], (h_codes, h_scales), g, w2_codes[w], j, PASSES2)

        def store(copy, b):
            cols = slice(BANK * b, BANK * (b + 1))
            copy(out=result[:, cols], in_=sums2[b][:])
            nc.sync.dma_start(out=out[:, cols], in_=result[:, cols])

        nc.vector.memset(start_flag[:], 1.0)
        for j in range(H // BANK):
            cols = slice(BANK * j, BANK * (j + 1))
            nc.vector.scalar_tensor_tensor(
                out=h[:, cols], in0=sums1[j][:], scalar=0.0, in1=ghb[:, cols], op0=MAX, op1=MULT
            )
        quantize_w2(0)
        h_words = h[:].bitcast(F32)
        h_banks = []
        for b in range(2):
            bank = psum.tile([P, 2, 2, TOKENS], F32, name="h_bank" + str(b), tag="x" + str(b))
            for g in range(2):
                for e in range(2):
                    base = 256 * (2 * b + g)
                    nc.tensor.transpose(bank[:, g, e, :], h_words[:, base + e : base + 256 : 2], ident32[:])
            h_banks.append(bank)
        load_w2(5)
        interleave_w2(2)
        quantize_w2(1)
        for b in range(2):
            words = h_grouped[:, 2 * b : 2 * b + 2, :].rearrange("p g x -> p (g x)").bitcast(F32)
            nc.scalar.copy(
                out=words.rearrange("p (g n e) -> p g n e", g=2, e=2), in_=h_banks[b][:].rearrange("p g e n -> p g n e")
            )
        load_w2(6)
        interleave_w2(3)
        for b in range(2):
            cols = slice(2 * TOKENS * b, 2 * TOKENS * (b + 1))
            nc.vector.quantize_mx(
                out=h_codes[:, cols].bitcast(FP8X4),
                scales=h_scales[:, cols],
                in_=h_grouped[:, 2 * b : 2 * b + 2, :].rearrange("p g x -> p (g x)"),
            )
        quantize_w2(2)

        for w in range(3):
            multiply_w2(w)
        load_w2(7)
        for w in range(4, 2 * PASSES2):
            interleave_w2(w)
            quantize_w2(w - 1)
            multiply_w2(w - 1)
        store(nc.scalar.copy, 0)
        store(nc.scalar.copy, 1)
        last = 2 * PASSES2 - 1
        w2_codes[last] = new_codes("w2", 4)
        for c0 in (0, BANK):
            quantize(w2_codes[last][0], w2_codes[last][1], w2_grouped[last], c0, c0 + BANK)
        multiply_w2(last)
        store(nc.scalar.copy, 2)
        store(nc.vector.tensor_copy, 3)
